import numpy as np
import ml_dtypes


def mxq(x, axis, fmt="e4m3"):
    dtype, down = {"e4m3": (ml_dtypes.float8_e4m3fn, 7), "e5m2": (ml_dtypes.float8_e5m2, 14)}[fmt]
    v = np.moveaxis(np.asarray(x, np.float32).astype(ml_dtypes.bfloat16).astype(np.float64), axis, -1)
    blocks = v.reshape(v.shape[:-1] + (-1, 32))
    amax = np.abs(blocks).max(-1, keepdims=True)
    byte = np.maximum(np.where(amax > 0, np.frexp(amax)[1] - 1 + 127, 0) - down, 1)
    scale = np.exp2(byte - 127.0)
    codes = (blocks / scale).astype(np.float32).astype(dtype).astype(np.float64)
    return np.moveaxis((codes * scale).reshape(v.shape), -1, axis)


WIDE = False


def mx_kscale(k):
    if not WIDE:
        return np.ones(k)
    levels = np.array([10, -10, 5, -5, 0])
    if k % 512:
        return np.exp2(np.random.permutation(np.resize(levels, k // 32))).repeat(32)
    a = np.empty((k // 512, 16))
    for p in range(k // 512):
        a[p, :8] = np.random.permutation(np.resize(levels, 8))
        for g in range(8):
            far = levels[np.abs(levels - a[p, g]) >= 10]
            a[p, g + 8] = far[np.random.randint(len(far))]
    return np.exp2(a.ravel()).repeat(32)


def f64(x):
    return np.asarray(x).astype(np.float64)


def striped(idx):
    return np.tile(idx.reshape(-1, 16).T, (8, 1)).astype(np.uint16)


def unstriped(offs):
    return offs[:16].T.reshape(-1).astype(np.int64)


def relu(v):
    return np.maximum(v, 0.0)


K, T, S, D, V, H, N, U = 512, 2048, 512, 3, 512, 512, 256, 1024
P = 2 ** 7


def setup_inputs():
    n = np.random.standard_normal
    s = mx_kscale(K)[:, None]
    u = mx_kscale(H)
    return {
        "xT": (n((K, T)) * s).astype(np.float32),
        "w1": (n((K, H)) / np.sqrt(K) / s * u).astype(np.float32),
        "w2": (n((H, N)) / np.sqrt(H) / u[:, None]).astype(np.float32),
        "gate": np.tile(np.random.uniform(0.2, 0.6, (D, 1, V)), (1, P, 1)).astype(np.float32),
        "emb": (0.5 * n((H, U)) * u[:, None]).astype(np.float32),
        "offs": striped(np.random.permutation(T)[:S]),
        "cell": striped(np.random.permutation(U)[:S]),
        "pos1": striped(np.random.permutation(U)[:V]),
        "pos2": striped(np.random.permutation(U)[:V]),
        "pos3": striped(np.random.permutation(U)[:V]),
    }


def reference(xT, w1, w2, gate, emb, offs, cell, pos1, pos2, pos3):
    xq = mxq(f64(xT)[:, unstriped(offs)], 0, "e4m3")
    up = np.zeros((H, U))
    up[:, unstriped(cell)] = relu(mxq(f64(w1), 0, "e4m3").T @ xq)
    z = up + f64(emb)
    y = relu(mxq(f64(w2), 0, "e4m3").T @ mxq(z, 0, "e4m3"))
    return y[:, unstriped(pos1)] * f64(gate)[0, :1] + y[:, unstriped(pos2)] * f64(gate)[1, :1] + y[:, unstriped(pos3)] * f64(gate)[2, :1]

@@ -1,0 +1,192 @@
+from contextlib import ExitStack
+
+import concourse.mybir as mybir
+from concourse.masks import make_identity
+
+K, T, S, D, V, H, N, U = 512, 2048, 512, 3, 512, 512, 256, 1024
+FLOPS = 2 * K * H * S + 2 * H * N * U
+
+F32 = mybir.dt.float32
+BF16 = mybir.dt.bfloat16
+U32 = mybir.dt.uint32
+U16 = mybir.dt.uint16
+U8 = mybir.dt.uint8
+FP8X4 = mybir.dt.float8_e4m3fn_x4
+ADD = mybir.AluOpType.add
+MULT = mybir.AluOpType.mult
+MAX = mybir.AluOpType.max
+RELU = mybir.ActivationFunctionType.Relu
+COPY = mybir.ActivationFunctionType.Copy
+
+P = 128
+PACK = 4
+HALF = S // 2
+CHUNK = 256
+CHUNKS = U // CHUNK
+
+
+def tile_picked_devox_relu_e_kernel(tc, xT, w1, w2, gate, emb, offs, cell, pos1, pos2, pos3, out):
+    nc = tc.nc
+    with ExitStack() as ctx:
+        keep = ctx.enter_context(tc.tile_pool(name="keep", bufs=1))
+        psum = ctx.enter_context(tc.psum_pool(name="psum", bufs=1))
+
+        def sb(name, shape, dtype):
+            return keep.tile(shape, dtype, name=name, align_bytes=64)
+
+        def bank(b, width):
+            return psum.tile([P, width], F32, name="bank%d" % b)
+
+        def load_list(name, src):
+            t = keep.tile([P, S // 16], U16, name=name)
+            nc.sync.dma_start(t[:], src)
+            return t
+
+        def quantize(codes, scales, values):
+            nc.vector.quantize_mx(out=codes.bitcast(FP8X4), scales=scales, in_=values)
+
+        def product(acc, w_codes, w_scales, a_codes, a_scales):
+            nc.tensor.matmul_mx(out=acc, lhsT=w_codes.bitcast(FP8X4), lhsT_scale=w_scales,
+                                rhs=a_codes.bitcast(FP8X4), rhs_scale=a_scales, start=True, stop=True)
+
+        x_rows = xT.rearrange("(p j) t -> p j t", j=PACK)
+        x_plane = [sb("x%d" % j, [P, T], F32) for j in range(PACK)]
+        w1_raw = sb("w1_raw", [P, PACK, H], F32)
+        nc.sync.dma_start(x_plane[0][:], x_rows[:, 0, :])
+        offs_t = load_list("offs_t", offs)
+        nc.sync.dma_start(w1_raw[:], w1.rearrange("(p j) c -> p j c", j=PACK))
+        for j in range(1, PACK):
+            nc.sync.dma_start(x_plane[j][:], x_rows[:, j, :])
+        cell_t = load_list("cell_t", cell)
+        emb_rows = emb.rearrange("(p t) r -> p t r", t=PACK)
+        emb_plane = [sb("emb%d" % t, [P, U], F32) for t in range(PACK)]
+        for t in range(PACK):
+            nc.sync.dma_start(emb_plane[t][:], emb_rows[:, t, :])
+        w2_raw = sb("w2_raw", [P, PACK, N], F32)
+        nc.sync.dma_start(w2_raw[:], w2.rearrange("(p j) c -> p j c", j=PACK))
+        pos_t = [load_list("pos%d_t" % d, src) for d, src in enumerate((pos1, pos2, pos3))]
+        gate_last = sb("gate_last", [P, V], F32)
+        nc.sync.dma_start(gate_last[:], gate[D - 1])
+        gate_col = [sb("gate_col%d" % d, [P, V // P], F32) for d in range(D - 1)]
+        with nc.allow_non_contiguous_dma("one weight a partition"):
+            for d in range(D - 1):
+                nc.sync.dma_start(gate_col[d][:], gate[d, 0, :].rearrange("(b p) -> p b", p=P))
+
+        ident = sb("ident", [P, P], F32)
+        make_identity(nc, ident[:])
+
+        up = [sb("up%d" % t, [P, U], F32) for t in range(PACK)]
+        for t in range(PACK):
+            nc.vector.memset(up[t][:], 0.0)
+
+        w1_bf = sb("w1_bf", [P, PACK * H], BF16)
+        nc.scalar.copy(w1_bf[:].rearrange("p (t m j) -> p m t j", t=PACK, j=PACK),
+                       w1_raw[:].rearrange("p j (m t) -> p m t j", t=PACK))
+        w1_codes = sb("w1_codes", [P, H], U32)
+        w1_scales = sb("w1_scales", [P, H], U8)
+        quantize(w1_codes[:], w1_scales[:], w1_bf[:])
+
+        x_bf = [sb("x_bf%d" % a, [P, HALF, PACK], BF16) for a in range(2)]
+        x_codes = sb("x_codes", [P, S], U32)
+        x_scales = sb("x_scales", [P, S], U8)
+
+        def half_cols(a):
+            return slice(a * HALF, (a + 1) * HALF)
+
+        def half_list(lst, a):
+            return lst[:, a * (HALF // 16):(a + 1) * (HALF // 16)]
+
+        for j in range(PACK):
+            for a in range(2):
+                nc.vector.tensor_copy(x_bf[a][:, :, j], x_plane[j][:].indirect(half_list(offs_t, a)))
+                if j == PACK - 1:
+                    quantize(x_codes[:, half_cols(a)], x_scales[:, half_cols(a)],
+                             x_bf[a][:].rearrange("p n j -> p (n j)"))
+
+        h = [sb("h%d" % t, [P, S], F32) for t in range(PACK)]
+        for a in range(2):
+            acc = bank(a, HALF)
+            product(acc[:], w1_codes[:, 0:P], w1_scales[:, 0:P], x_codes[:, half_cols(a)], x_scales[:, half_cols(a)])
+            nc.scalar.activation(h[0][:, half_cols(a)], acc[:], RELU)
+            nc.vector.tensor_copy(up[0][:].indirect(half_list(cell_t, a)), h[0][:, half_cols(a)])
+        for t in range(1, PACK):
+            acc = bank(1 + t, S)
+            cols = slice(t * P, (t + 1) * P)
+            product(acc[:], w1_codes[:, cols], w1_scales[:, cols], x_codes[:], x_scales[:])
+            nc.scalar.activation(h[t][:], acc[:], RELU)
+            nc.vector.tensor_copy(up[t][:].indirect(cell_t[:]), h[t][:])
+
+        w2_bf = sb("w2_bf", [P, N, PACK], BF16)
+        nc.scalar.copy(w2_bf[:], w2_raw[:].rearrange("p j c -> p c j"))
+        w2_codes = sb("w2_codes", [P, N], U32)
+        w2_scales = sb("w2_scales", [P, N], U8)
+        quantize(w2_codes[:], w2_scales[:], w2_bf[:].rearrange("p c j -> p (c j)"))
+
+        def chunk_cols(c):
+            return slice(c * CHUNK, (c + 1) * CHUNK)
+
+        z_early = sb("z_early", [P, 2, U], BF16)
+        z_third = sb("z_third", [P, U], BF16)
+        pairs = sb("pairs", [P, PACK * U], BF16)
+        pairs_v = pairs[:].rearrange("p (c u r e) -> p c u r e", c=CHUNKS, u=2, e=2)
+        for t in range(2):
+            nc.gpsimd.tensor_tensor(z_early[:, t, :], up[t][:], emb_plane[t][:], ADD)
+        nc.scalar.copy(pairs_v[:, :, 0, :, :], z_early[:].rearrange("p e (c r) -> p c r e", c=CHUNKS))
+        for c in range(CHUNKS):
+            nc.gpsimd.tensor_tensor(z_third[:, chunk_cols(c)], up[2][:, chunk_cols(c)], emb_plane[2][:, chunk_cols(c)], ADD)
+            nc.scalar.copy(pairs_v[:, c, 1, :, :], z_third[:, chunk_cols(c)].unsqueeze(2).to_broadcast([P, CHUNK, 2]))
+        for c in range(CHUNKS):
+            nc.vector.tensor_tensor(pairs_v[:, c, 1, :, 1], up[3][:, chunk_cols(c)], emb_plane[3][:, chunk_cols(c)], ADD)
+
+        z_codes = sb("z_codes", [P, U], U32)
+        z_scales = sb("z_scales", [P, U], U8)
+        y = [sb("y%d" % m, [P, U], F32) for m in range(2)]
+        words = pairs[:].bitcast(F32)
+        z_bf = [sb("z_bf%d" % c, [P, PACK * CHUNK], BF16) for c in range(CHUNKS)]
+        for c in range(CHUNKS):
+            src = words[:, c * 2 * CHUNK:(c + 1) * 2 * CHUNK].rearrange("p (u r) -> p r u", u=2)
+            dst = z_bf[c][:].bitcast(F32).rearrange("p (r u) -> p r u", u=2)
+            if c < CHUNKS - 1:
+                nc.scalar.copy(dst, src)
+            else:
+                nc.vector.tensor_copy(dst, src)
+        for c in range(CHUNKS):
+            quantize(z_codes[:, chunk_cols(c)], z_scales[:, chunk_cols(c)], z_bf[c][:])
+            acc = bank((5 + c) % 8, CHUNK)
+            product(acc[:], w2_codes[:, 0:P], w2_scales[:, 0:P], z_codes[:, chunk_cols(c)], z_scales[:, chunk_cols(c)])
+            if c < CHUNKS - 1:
+                nc.scalar.activation(y[0][:, chunk_cols(c)], acc[:], RELU)
+            else:
+                nc.vector.tensor_scalar(y[0][:, chunk_cols(c)], acc[:], 0.0, None, MAX)
+        for a in range(2):
+            cols = slice(a * (U // 2), (a + 1) * (U // 2))
+            acc = bank(1 + a, U // 2)
+            product(acc[:], w2_codes[:, P:2 * P], w2_scales[:, P:2 * P], z_codes[:, cols], z_scales[:, cols])
+            nc.scalar.activation(y[1][:, cols], acc[:], RELU)
+
+        partial = []
+        for m in range(2):
+            scaled = []
+            for d in range(D - 1):
+                picked = sb("picked%d%d" % (m, d), [P, V], F32)
+                nc.vector.tensor_copy(picked[:], y[m][:].indirect(pos_t[d][:]))
+                turned = bank(3 + 2 * m + d, V)
+                for b in range(V // P):
+                    nc.tensor.transpose(turned[:, b * P:(b + 1) * P], picked[:, b * P:(b + 1) * P], ident[:])
+                s = sb("scaled%d%d" % (m, d), [P, V], F32)
+                for b in range(V // P):
+                    nc.scalar.activation(s[:, b * P:(b + 1) * P], turned[:, b * P:(b + 1) * P], COPY,
+                                         scale=gate_col[d][:, b:b + 1])
+                scaled.append(s)
+            acc = bank((7 + m) % 8, V)
+            for b in range(V // P):
+                for d in range(D - 1):
+                    nc.tensor.matmul(acc[:, b * P:(b + 1) * P], scaled[d][:, b * P:(b + 1) * P], ident[:],
+                                     start=(d == 0), stop=(d == D - 2), is_transpose=True)
+            partial.append(acc)
+        for m in range(2):
+            last = sb("last%d" % m, [P, V], F32)
+            nc.vector.tensor_tensor(last[:], y[m][:].indirect(pos_t[D - 1][:]), gate_last[:], MULT)
+            res = sb("res%d" % m, [P, V], F32)
+            nc.vector.tensor_tensor(res[:], last[:], partial[m][:], ADD)
+            nc.sync.dma_start(out[m * P:(m + 1) * P, :], res[:])

@@ -23,6 +23,7 @@ PACK = 4
 HALF = S // 2
 CHUNK = 256
 CHUNKS = U // CHUNK
+ORDER = (2, 0, 1, 3)
 
 
 def tile_picked_devox_relu_e_kernel(tc, xT, w1, w2, gate, emb, offs, cell, pos1, pos2, pos3, out):
@@ -51,22 +52,25 @@ def tile_picked_devox_relu_e_kernel(tc, xT, w1, w2, gate, emb, offs, cell, pos1,
 
         x_rows = xT.rearrange("(p j) t -> p j t", j=PACK)
         x_plane = [sb("x%d" % j, [P, T], F32) for j in range(PACK)]
-        w1_raw = sb("w1_raw", [P, PACK, H], F32)
+        w1_rows = w1.rearrange("(p j) c -> p j c", j=PACK)
+        w1_raw = [sb("w1_raw%d" % a, [P, PACK, H // 2], F32) for a in range(2)]
         nc.sync.dma_start(x_plane[0][:], x_rows[:, 0, :])
         offs_t = load_list("offs_t", offs)
-        nc.sync.dma_start(w1_raw[:], w1.rearrange("(p j) c -> p j c", j=PACK))
         for j in range(1, PACK):
             nc.sync.dma_start(x_plane[j][:], x_rows[:, j, :])
+        for a in range(2):
+            nc.sync.dma_start(w1_raw[a][:], w1_rows[:, :, a * (H // 2):(a + 1) * (H // 2)])
         cell_t = load_list("cell_t", cell)
         emb_rows = emb.rearrange("(p t) r -> p t r", t=PACK)
         emb_plane = [sb("emb%d" % t, [P, U], F32) for t in range(PACK)]
-        for t in range(PACK):
+        for t in ORDER:
             nc.sync.dma_start(emb_plane[t][:], emb_rows[:, t, :])
         w2_raw = sb("w2_raw", [P, PACK, N], F32)
         nc.sync.dma_start(w2_raw[:], w2.rearrange("(p j) c -> p j c", j=PACK))
         pos_t = [load_list("pos%d_t" % d, src) for d, src in enumerate((pos1, pos2, pos3))]
-        gate_last = sb("gate_last", [P, V], F32)
-        nc.sync.dma_start(gate_last[:], gate[D - 1])
+        gate_row = [sb("gate_row%d" % d, [P, V], F32) for d in range(D)]
+        for d in range(D):
+            nc.sync.dma_start(gate_row[d][:], gate[d])
         gate_col = [sb("gate_col%d" % d, [P, V // P], F32) for d in range(D - 1)]
         with nc.allow_non_contiguous_dma("one weight a partition"):
             for d in range(D - 1):
@@ -78,13 +82,6 @@ def tile_picked_devox_relu_e_kernel(tc, xT, w1, w2, gate, emb, offs, cell, pos1,
         up = [sb("up%d" % t, [P, U], F32) for t in range(PACK)]
         for t in range(PACK):
             nc.vector.memset(up[t][:], 0.0)
-
-        w1_bf = sb("w1_bf", [P, PACK * H], BF16)
-        nc.scalar.copy(w1_bf[:].rearrange("p (t m j) -> p m t j", t=PACK, j=PACK),
-                       w1_raw[:].rearrange("p j (m t) -> p m t j", t=PACK))
-        w1_codes = sb("w1_codes", [P, H], U32)
-        w1_scales = sb("w1_scales", [P, H], U8)
-        quantize(w1_codes[:], w1_scales[:], w1_bf[:])
 
         x_bf = [sb("x_bf%d" % a, [P, HALF, PACK], BF16) for a in range(2)]
         x_codes = sb("x_codes", [P, S], U32)
@@ -103,90 +100,109 @@ def tile_picked_devox_relu_e_kernel(tc, xT, w1, w2, gate, emb, offs, cell, pos1,
                     quantize(x_codes[:, half_cols(a)], x_scales[:, half_cols(a)],
                              x_bf[a][:].rearrange("p n j -> p (n j)"))
 
+        w1_bf = sb("w1_bf", [P, PACK * H], BF16)
+        w1_dealt = w1_bf[:].rearrange("p (t m j) -> p m t j", t=PACK, j=PACK)
+        nc.scalar.copy(w1_dealt[:, 0:P // 2], w1_raw[0][:].rearrange("p j (m t) -> p m t j", t=PACK))
+        nc.vector.tensor_copy(w1_dealt[:, P // 2:P], w1_raw[1][:].rearrange("p j (m t) -> p m t j", t=PACK))
+        w1_codes = sb("w1_codes", [P, H], U32)
+        w1_scales = sb("w1_scales", [P, H], U8)
+        for lo, hi in ((2, 3), (0, 2), (3, 4)):
+            quantize(w1_codes[:, lo * P:hi * P], w1_scales[:, lo * P:hi * P], w1_bf[:, lo * H:hi * H])
+
         h = [sb("h%d" % t, [P, S], F32) for t in range(PACK)]
+        first = ORDER[0]
+        cols = slice(first * P, (first + 1) * P)
         for a in range(2):
             acc = bank(a, HALF)
-            product(acc[:], w1_codes[:, 0:P], w1_scales[:, 0:P], x_codes[:, half_cols(a)], x_scales[:, half_cols(a)])
-            nc.scalar.activation(h[0][:, half_cols(a)], acc[:], RELU)
-            nc.vector.tensor_copy(up[0][:].indirect(half_list(cell_t, a)), h[0][:, half_cols(a)])
-        for t in range(1, PACK):
-            acc = bank(1 + t, S)
+            product(acc[:], w1_codes[:, cols], w1_scales[:, cols], x_codes[:, half_cols(a)], x_scales[:, half_cols(a)])
+            nc.scalar.activation(h[first][:, half_cols(a)], acc[:], RELU)
+            nc.vector.tensor_copy(up[first][:].indirect(half_list(cell_t, a)), h[first][:, half_cols(a)])
+        for i, t in enumerate(ORDER[1:]):
+            acc = bank(2 + i, S)
             cols = slice(t * P, (t + 1) * P)
             product(acc[:], w1_codes[:, cols], w1_scales[:, cols], x_codes[:], x_scales[:])
             nc.scalar.activation(h[t][:], acc[:], RELU)
             nc.vector.tensor_copy(up[t][:].indirect(cell_t[:]), h[t][:])
 
-        w2_bf = sb("w2_bf", [P, N, PACK], BF16)
-        nc.scalar.copy(w2_bf[:], w2_raw[:].rearrange("p j c -> p c j"))
-        w2_codes = sb("w2_codes", [P, N], U32)
-        w2_scales = sb("w2_scales", [P, N], U8)
-        quantize(w2_codes[:], w2_scales[:], w2_bf[:].rearrange("p c j -> p (c j)"))
-
         def chunk_cols(c):
             return slice(c * CHUNK, (c + 1) * CHUNK)
 
-        z_early = sb("z_early", [P, 2, U], BF16)
-        z_third = sb("z_third", [P, U], BF16)
-        pairs = sb("pairs", [P, PACK * U], BF16)
-        pairs_v = pairs[:].rearrange("p (c u r e) -> p c u r e", c=CHUNKS, u=2, e=2)
+        w2_bf = sb("w2_bf", [P, N, PACK], BF16)
+        nc.scalar.copy(w2_bf[:], w2_raw[:].rearrange("p j c -> p c j"))
+
+        z_plane = [sb("z_plane%d" % t, [P, U], BF16) for t in range(PACK - 1)]
+        pairs = [sb("pairs%d" % c, [P, 2, CHUNK, 2], BF16) for c in range(CHUNKS)]
+        nc.gpsimd.tensor_tensor(z_plane[2][:], up[2][:], emb_plane[2][:], ADD)
+        for c in range(CHUNKS):
+            nc.scalar.copy(pairs[c][:, 1, :, :], z_plane[2][:, chunk_cols(c)].unsqueeze(2).to_broadcast([P, CHUNK, 2]))
         for t in range(2):
-            nc.gpsimd.tensor_tensor(z_early[:, t, :], up[t][:], emb_plane[t][:], ADD)
-        nc.scalar.copy(pairs_v[:, :, 0, :, :], z_early[:].rearrange("p e (c r) -> p c r e", c=CHUNKS))
+            for a in range(1 + t):
+                cols = slice(a * (U // (1 + t)), (a + 1) * (U // (1 + t)))
+                nc.gpsimd.tensor_tensor(z_plane[t][:, cols], up[t][:, cols], emb_plane[t][:, cols], ADD)
+            for c in range(CHUNKS):
+                nc.scalar.copy(pairs[c][:, 0, :, t], z_plane[t][:, chunk_cols(c)])
         for c in range(CHUNKS):
-            nc.gpsimd.tensor_tensor(z_third[:, chunk_cols(c)], up[2][:, chunk_cols(c)], emb_plane[2][:, chunk_cols(c)], ADD)
-            nc.scalar.copy(pairs_v[:, c, 1, :, :], z_third[:, chunk_cols(c)].unsqueeze(2).to_broadcast([P, CHUNK, 2]))
-        for c in range(CHUNKS):
-            nc.vector.tensor_tensor(pairs_v[:, c, 1, :, 1], up[3][:, chunk_cols(c)], emb_plane[3][:, chunk_cols(c)], ADD)
+            nc.vector.tensor_tensor(pairs[c][:, 1, :, 1], up[3][:, chunk_cols(c)], emb_plane[3][:, chunk_cols(c)], ADD)
+
+        w2_codes = sb("w2_codes", [P, N], U32)
+        w2_scales = sb("emb3", [P, N], U8)
+        quantize(w2_codes[:], w2_scales[:], w2_bf[:].rearrange("p c j -> p (c j)"))
 
         z_codes = sb("z_codes", [P, U], U32)
         z_scales = sb("z_scales", [P, U], U8)
-        y = [sb("y%d" % m, [P, U], F32) for m in range(2)]
-        words = pairs[:].bitcast(F32)
-        z_bf = [sb("z_bf%d" % c, [P, PACK * CHUNK], BF16) for c in range(CHUNKS)]
+        z_bf = [sb("z_plane1" if c == 0 else "z_bf%d" % c, [P, PACK * CHUNK], BF16) for c in range(CHUNKS)]
         for c in range(CHUNKS):
-            src = words[:, c * 2 * CHUNK:(c + 1) * 2 * CHUNK].rearrange("p (u r) -> p r u", u=2)
-            dst = z_bf[c][:].bitcast(F32).rearrange("p (r u) -> p r u", u=2)
-            if c < CHUNKS - 1:
-                nc.scalar.copy(dst, src)
-            else:
-                nc.vector.tensor_copy(dst, src)
+            words = pairs[c][:].rearrange("p u r e -> p (u r e)").bitcast(F32)
+            nc.scalar.copy(z_bf[c][:].bitcast(F32).rearrange("p (r u) -> p r u", u=2),
+                           words.rearrange("p (u r) -> p r u", u=2))
         for c in range(CHUNKS):
             quantize(z_codes[:, chunk_cols(c)], z_scales[:, chunk_cols(c)], z_bf[c][:])
-            acc = bank((5 + c) % 8, CHUNK)
+        y = [sb(name, [P, U], F32) for name in ("pairs3", "y1")]
+        for c in range(CHUNKS):
+            acc = bank(4 + c, CHUNK)
             product(acc[:], w2_codes[:, 0:P], w2_scales[:, 0:P], z_codes[:, chunk_cols(c)], z_scales[:, chunk_cols(c)])
-            if c < CHUNKS - 1:
+            if c in (0, CHUNKS - 1):
                 nc.scalar.activation(y[0][:, chunk_cols(c)], acc[:], RELU)
             else:
                 nc.vector.tensor_scalar(y[0][:, chunk_cols(c)], acc[:], 0.0, None, MAX)
         for a in range(2):
             cols = slice(a * (U // 2), (a + 1) * (U // 2))
-            acc = bank(1 + a, U // 2)
+            acc = bank(5 + a, U // 2)
             product(acc[:], w2_codes[:, P:2 * P], w2_scales[:, P:2 * P], z_codes[:, cols], z_scales[:, cols])
             nc.scalar.activation(y[1][:, cols], acc[:], RELU)
 
-        partial = []
+        picked = [[sb("picked%d%d" % (m, d), [P, V], F32) for d in range(D - 1)] for m in range(2)]
         for m in range(2):
-            scaled = []
             for d in range(D - 1):
-                picked = sb("picked%d%d" % (m, d), [P, V], F32)
-                nc.vector.tensor_copy(picked[:], y[m][:].indirect(pos_t[d][:]))
-                turned = bank(3 + 2 * m + d, V)
-                for b in range(V // P):
-                    nc.tensor.transpose(turned[:, b * P:(b + 1) * P], picked[:, b * P:(b + 1) * P], ident[:])
-                s = sb("scaled%d%d" % (m, d), [P, V], F32)
-                for b in range(V // P):
-                    nc.scalar.activation(s[:, b * P:(b + 1) * P], turned[:, b * P:(b + 1) * P], COPY,
-                                         scale=gate_col[d][:, b:b + 1])
-                scaled.append(s)
-            acc = bank((7 + m) % 8, V)
+                nc.vector.tensor_copy(picked[m][d][:], y[m][:].indirect(pos_t[d][:]))
+
+        weighted = [sb("weighted%d" % d, [P, V], F32) for d in range(D - 1)]
+        for d in range(D - 1):
+            nc.gpsimd.tensor_tensor(weighted[d][:], picked[0][d][:], gate_row[d][:], MULT)
+        partial0 = sb("partial0", [P, V], F32)
+        nc.gpsimd.tensor_tensor(partial0[:], weighted[0][:], weighted[1][:], ADD)
+
+        scaled = []
+        for d in range(D - 1):
+            turned = bank(d, V)
             for b in range(V // P):
-                for d in range(D - 1):
-                    nc.tensor.matmul(acc[:, b * P:(b + 1) * P], scaled[d][:, b * P:(b + 1) * P], ident[:],
-                                     start=(d == 0), stop=(d == D - 2), is_transpose=True)
-            partial.append(acc)
-        for m in range(2):
-            last = sb("last%d" % m, [P, V], F32)
-            nc.vector.tensor_tensor(last[:], y[m][:].indirect(pos_t[D - 1][:]), gate_last[:], MULT)
+                nc.tensor.transpose(turned[:, b * P:(b + 1) * P], picked[1][d][:, b * P:(b + 1) * P], ident[:])
+            s = sb("scaled%d" % d, [P, V], F32)
+            for b in range(V // P):
+                nc.scalar.activation(s[:, b * P:(b + 1) * P], turned[:, b * P:(b + 1) * P], COPY,
+                                     scale=gate_col[d][:, b:b + 1])
+            scaled.append(s)
+        partial1 = bank(2, V)
+        for b in range(V // P):
+            for d in range(D - 1):
+                nc.tensor.matmul(partial1[:, b * P:(b + 1) * P], scaled[d][:, b * P:(b + 1) * P], ident[:],
+                                 start=(d == 0), stop=(d == D - 2), is_transpose=True)
+        for m, partial in enumerate((partial0, partial1)):
+            last = sb("weighted0", [P, V], F32)
+            nc.vector.tensor_tensor(last[:], y[m][:].indirect(pos_t[D - 1][:]), gate_row[D - 1][:], MULT)
             res = sb("res%d" % m, [P, V], F32)
-            nc.vector.tensor_tensor(res[:], last[:], partial[m][:], ADD)
-            nc.sync.dma_start(out[m * P:(m + 1) * P, :], res[:])
+            pieces = 1 + m
+            for a in range(pieces):
+                cols = slice(a * (V // pieces), (a + 1) * (V // pieces))
+                nc.vector.tensor_tensor(res[:, cols], last[:, cols], partial[:, cols], ADD)
+                nc.sync.dma_start(out[m * P:(m + 1) * P, cols], res[:, cols])

@@ -71,9 +71,9 @@ def tile_picked_devox_relu_e_kernel(tc, xT, w1, w2, gate, emb, offs, cell, pos1,
         gate_row = [sb("gate_row%d" % d, [P, V], F32) for d in range(D)]
         for d in range(D):
             nc.sync.dma_start(gate_row[d][:], gate[d])
-        gate_col = [sb("gate_col%d" % d, [P, V // P], F32) for d in range(D - 1)]
+        gate_col = [sb("gate_col%d" % d, [P, V // P], F32) for d in range(D)]
         with nc.allow_non_contiguous_dma("one weight a partition"):
-            for d in range(D - 1):
+            for d in range(D):
                 nc.sync.dma_start(gate_col[d][:], gate[d, 0, :].rearrange("(b p) -> p b", p=P))
 
         ident = sb("ident", [P, P], F32)
@@ -102,12 +102,21 @@ def tile_picked_devox_relu_e_kernel(tc, xT, w1, w2, gate, emb, offs, cell, pos1,
 
         w1_bf = sb("w1_bf", [P, PACK * H], BF16)
         w1_dealt = w1_bf[:].rearrange("p (t m j) -> p m t j", t=PACK, j=PACK)
-        nc.scalar.copy(w1_dealt[:, 0:P // 2], w1_raw[0][:].rearrange("p j (m t) -> p m t j", t=PACK))
-        nc.vector.tensor_copy(w1_dealt[:, P // 2:P], w1_raw[1][:].rearrange("p j (m t) -> p m t j", t=PACK))
+        w1_early = w1_raw[0][:].rearrange("p j (m t) -> p m t j", t=PACK)
+        w1_late = w1_raw[1][:].rearrange("p j (m t) -> p m t j", t=PACK)
         w1_codes = sb("w1_codes", [P, H], U32)
         w1_scales = sb("w1_scales", [P, H], U8)
-        for lo, hi in ((2, 3), (0, 2), (3, 4)):
+        def quantize_w1(lo, hi):
             quantize(w1_codes[:, lo * P:hi * P], w1_scales[:, lo * P:hi * P], w1_bf[:, lo * H:hi * H])
+
+        for lo, hi in ((2, 3), (0, 2), (3, 4)):
+            nc.scalar.copy(w1_dealt[:, 0:P // 2, lo:hi], w1_early[:, :, lo:hi])
+        nc.vector.tensor_copy(w1_dealt[:, P // 2:P, 2:3], w1_late[:, :, 2:3])
+        quantize_w1(2, 3)
+        nc.vector.tensor_copy(w1_dealt[:, P // 2:P, 3:4], w1_late[:, :, 3:4])
+        nc.vector.tensor_copy(w1_dealt[:, P // 2:P, 0:2], w1_late[:, :, 0:2])
+        quantize_w1(0, 2)
+        quantize_w1(3, 4)
 
         h = [sb("h%d" % t, [P, S], F32) for t in range(PACK)]
         first = ORDER[0]
@@ -144,65 +153,83 @@ def tile_picked_devox_relu_e_kernel(tc, xT, w1, w2, gate, emb, offs, cell, pos1,
         for c in range(CHUNKS):
             nc.vector.tensor_tensor(pairs[c][:, 1, :, 1], up[3][:, chunk_cols(c)], emb_plane[3][:, chunk_cols(c)], ADD)
 
-        w2_codes = sb("w2_codes", [P, N], U32)
-        w2_scales = sb("emb3", [P, N], U8)
-        quantize(w2_codes[:], w2_scales[:], w2_bf[:].rearrange("p c j -> p (c j)"))
+        def quantize_w2(m, after):
+            codes = sb("w2_codes%d" % m, [P, P], U32)
+            scales = sb(after, [P, P], U8)
+            quantize(codes[:], scales[:], w2_bf[:, m * P:(m + 1) * P, :].rearrange("p c j -> p (c j)"))
+            return codes, scales
+
+        w2_first = quantize_w2(0, "emb3")
 
         z_codes = sb("z_codes", [P, U], U32)
         z_scales = sb("z_scales", [P, U], U8)
         z_bf = [sb("z_plane1" if c == 0 else "z_bf%d" % c, [P, PACK * CHUNK], BF16) for c in range(CHUNKS)]
         for c in range(CHUNKS):
             words = pairs[c][:].rearrange("p u r e -> p (u r e)").bitcast(F32)
-            nc.scalar.copy(z_bf[c][:].bitcast(F32).rearrange("p (r u) -> p r u", u=2),
-                           words.rearrange("p (u r) -> p r u", u=2))
+            src = words.rearrange("p (u r) -> p r u", u=2)
+            dst = z_bf[c][:].bitcast(F32).rearrange("p (r u) -> p r u", u=2)
+            if c < CHUNKS - 1:
+                nc.scalar.copy(dst, src)
+            else:
+                nc.scalar.copy(dst[:, 0:CHUNK // 2], src[:, 0:CHUNK // 2])
+                nc.vector.tensor_copy(dst[:, CHUNK // 2:CHUNK], src[:, CHUNK // 2:CHUNK])
         for c in range(CHUNKS):
             quantize(z_codes[:, chunk_cols(c)], z_scales[:, chunk_cols(c)], z_bf[c][:])
         y = [sb(name, [P, U], F32) for name in ("pairs3", "y1")]
-        for c in range(CHUNKS):
-            acc = bank(4 + c, CHUNK)
-            product(acc[:], w2_codes[:, 0:P], w2_scales[:, 0:P], z_codes[:, chunk_cols(c)], z_scales[:, chunk_cols(c)])
-            if c in (0, CHUNKS - 1):
-                nc.scalar.activation(y[0][:, chunk_cols(c)], acc[:], RELU)
+        pieces = ((0, 256, 4, False), (256, 512, 5, False), (512, 768, 6, True), (768, 896, 7, False), (896, 1024, 3, True))
+        for lo, hi, b, on_vector in pieces:
+            acc = bank(b, hi - lo)
+            product(acc[:], w2_first[0][:], w2_first[1][:], z_codes[:, lo:hi], z_scales[:, lo:hi])
+            if on_vector:
+                nc.vector.tensor_scalar(y[0][:, lo:hi], acc[:], 0.0, None, MAX)
             else:
-                nc.vector.tensor_scalar(y[0][:, chunk_cols(c)], acc[:], 0.0, None, MAX)
+                nc.scalar.activation(y[0][:, lo:hi], acc[:], RELU)
+        w2_second = quantize_w2(1, "z_bf3")
         for a in range(2):
             cols = slice(a * (U // 2), (a + 1) * (U // 2))
-            acc = bank(5 + a, U // 2)
-            product(acc[:], w2_codes[:, P:2 * P], w2_scales[:, P:2 * P], z_codes[:, cols], z_scales[:, cols])
+            acc = bank(6 + a, U // 2)
+            product(acc[:], w2_second[0][:], w2_second[1][:], z_codes[:, cols], z_scales[:, cols])
             nc.scalar.activation(y[1][:, cols], acc[:], RELU)
 
-        picked = [[sb("picked%d%d" % (m, d), [P, V], F32) for d in range(D - 1)] for m in range(2)]
-        for m in range(2):
-            for d in range(D - 1):
-                nc.vector.tensor_copy(picked[m][d][:], y[m][:].indirect(pos_t[d][:]))
-
-        weighted = [sb("weighted%d" % d, [P, V], F32) for d in range(D - 1)]
+        weighted = []
         for d in range(D - 1):
-            nc.gpsimd.tensor_tensor(weighted[d][:], picked[0][d][:], gate_row[d][:], MULT)
-        partial0 = sb("partial0", [P, V], F32)
-        nc.gpsimd.tensor_tensor(partial0[:], weighted[0][:], weighted[1][:], ADD)
+            picked = sb("picked0%d" % d, [P, V], F32)
+            nc.vector.tensor_copy(picked[:], y[0][:].indirect(pos_t[d][:]))
+            w = sb("weighted%d" % d, [P, V], F32)
+            nc.gpsimd.tensor_tensor(w[:], picked[:], gate_row[d][:], MULT)
+            weighted.append(w)
+        partial = sb("partial", [P, V], F32)
+        nc.gpsimd.tensor_tensor(partial[:], weighted[0][:], weighted[1][:], ADD)
 
-        scaled = []
-        for d in range(D - 1):
-            turned = bank(d, V)
-            for b in range(V // P):
-                nc.tensor.transpose(turned[:, b * P:(b + 1) * P], picked[1][d][:, b * P:(b + 1) * P], ident[:])
-            s = sb("scaled%d" % d, [P, V], F32)
-            for b in range(V // P):
-                nc.scalar.activation(s[:, b * P:(b + 1) * P], turned[:, b * P:(b + 1) * P], COPY,
-                                     scale=gate_col[d][:, b:b + 1])
-            scaled.append(s)
-        partial1 = bank(2, V)
-        for b in range(V // P):
-            for d in range(D - 1):
-                nc.tensor.matmul(partial1[:, b * P:(b + 1) * P], scaled[d][:, b * P:(b + 1) * P], ident[:],
-                                 start=(d == 0), stop=(d == D - 2), is_transpose=True)
-        for m, partial in enumerate((partial0, partial1)):
-            last = sb("weighted0", [P, V], F32)
-            nc.vector.tensor_tensor(last[:], y[m][:].indirect(pos_t[D - 1][:]), gate_row[D - 1][:], MULT)
-            res = sb("res%d" % m, [P, V], F32)
-            pieces = 1 + m
-            for a in range(pieces):
-                cols = slice(a * (V // pieces), (a + 1) * (V // pieces))
-                nc.vector.tensor_tensor(res[:, cols], last[:, cols], partial[:, cols], ADD)
-                nc.sync.dma_start(out[m * P:(m + 1) * P, cols], res[:, cols])
+        total = [bank(b, V // 2) for b in (4, 5)]
+        for d in range(D):
+            picked = sb("picked1%d" % d, [P, V], F32)
+            if d < D - 1:
+                nc.vector.tensor_copy(picked[:], y[1][:].indirect(pos_t[d][:]))
+            else:
+                for a in range(2):
+                    nc.vector.tensor_copy(picked[:, half_cols(a)], y[1][:].indirect(half_list(pos_t[d], a)))
+            scaled = sb("scaled%d" % d, [P, V], F32)
+            for a in range(2):
+                turned = bank(2 * (d % 2) + a, V // 2)
+                for i in range(2):
+                    b = 2 * a + i
+                    nc.tensor.transpose(turned[:, i * P:(i + 1) * P], picked[:, b * P:(b + 1) * P], ident[:])
+                for i in range(2):
+                    b = 2 * a + i
+                    nc.scalar.activation(scaled[:, b * P:(b + 1) * P], turned[:, i * P:(i + 1) * P], COPY,
+                                         scale=gate_col[d][:, b:b + 1])
+            for a in range(2):
+                for i in range(2):
+                    b = 2 * a + i
+                    nc.tensor.matmul(total[a][:, i * P:(i + 1) * P], scaled[:, b * P:(b + 1) * P], ident[:],
+                                     start=(d == 0 and i == 0), stop=(d == D - 1 and i == 1), is_transpose=True)
+        last = sb("weighted0", [P, V], F32)
+        nc.vector.tensor_tensor(last[:], y[0][:].indirect(pos_t[D - 1][:]), gate_row[D - 1][:], MULT)
+        res = [sb("res%d" % m, [P, V], F32) for m in range(2)]
+        for a in range(2):
+            cols = slice(a * (V // 2), (a + 1) * (V // 2))
+            nc.vector.tensor_tensor(res[0][:, cols], last[:, cols], partial[:, cols], ADD)
+            nc.sync.dma_start(out[0:P, cols], res[0][:, cols])
+            nc.scalar.copy(res[1][:, cols], total[a][:])
+            nc.scalar.dma_start(out[P:2 * P, cols], res[1][:, cols])

@@ -71,10 +71,11 @@ def tile_picked_devox_relu_e_kernel(tc, xT, w1, w2, gate, emb, offs, cell, pos1,
         gate_row = [sb("gate_row%d" % d, [P, V], F32) for d in range(D)]
         for d in range(D):
             nc.sync.dma_start(gate_row[d][:], gate[d])
-        gate_col = [sb("gate_col%d" % d, [P, V // P], F32) for d in range(D)]
+        blocks = [V // P, V // P, HALF // P]
+        gate_col = [sb("gate_col%d" % d, [P, blocks[d]], F32) for d in range(D)]
         with nc.allow_non_contiguous_dma("one weight a partition"):
             for d in range(D):
-                nc.sync.dma_start(gate_col[d][:], gate[d, 0, :].rearrange("(b p) -> p b", p=P))
+                nc.sync.dma_start(gate_col[d][:], gate[d, 0, 0:blocks[d] * P].rearrange("(b p) -> p b", p=P))
 
         ident = sb("ident", [P, P], F32)
         make_identity(nc, ident[:])
@@ -139,6 +140,20 @@ def tile_picked_devox_relu_e_kernel(tc, xT, w1, w2, gate, emb, offs, cell, pos1,
         w2_bf = sb("w2_bf", [P, N, PACK], BF16)
         nc.scalar.copy(w2_bf[:], w2_raw[:].rearrange("p j c -> p c j"))
 
+        emb_turned = sb("emb_turned", [P, (CHUNKS - 1) * CHUNK], F32)
+        emb_psum = []
+        for c in range(CHUNKS - 1):
+            there = bank(5 + c, CHUNK)
+            back = bank(c, CHUNK)
+            for i in range(2):
+                b = 2 * c + i
+                nc.tensor.transpose(there[:, i * P:(i + 1) * P], emb_plane[3][:, b * P:(b + 1) * P], ident[:])
+            nc.scalar.copy(emb_turned[:, chunk_cols(c)], there[:])
+            for i in range(2):
+                b = 2 * c + i
+                nc.tensor.transpose(back[:, i * P:(i + 1) * P], emb_turned[:, b * P:(b + 1) * P], ident[:])
+            emb_psum.append(back)
+
         z_plane = [sb("z_plane%d" % t, [P, U], BF16) for t in range(PACK - 1)]
         pairs = [sb("pairs%d" % c, [P, 2, CHUNK, 2], BF16) for c in range(CHUNKS)]
         nc.gpsimd.tensor_tensor(z_plane[2][:], up[2][:], emb_plane[2][:], ADD)
@@ -150,8 +165,10 @@ def tile_picked_devox_relu_e_kernel(tc, xT, w1, w2, gate, emb, offs, cell, pos1,
                 nc.gpsimd.tensor_tensor(z_plane[t][:, cols], up[t][:, cols], emb_plane[t][:, cols], ADD)
             for c in range(CHUNKS):
                 nc.scalar.copy(pairs[c][:, 0, :, t], z_plane[t][:, chunk_cols(c)])
-        for c in range(CHUNKS):
-            nc.vector.tensor_tensor(pairs[c][:, 1, :, 1], up[3][:, chunk_cols(c)], emb_plane[3][:, chunk_cols(c)], ADD)
+        for c in range(CHUNKS - 1):
+            nc.vector.tensor_tensor(pairs[c][:, 1, :, 1], up[3][:, chunk_cols(c)], emb_psum[c][:], ADD)
+        c = CHUNKS - 1
+        nc.gpsimd.tensor_tensor(pairs[c][:, 1, :, 1], up[3][:, chunk_cols(c)], emb_plane[3][:, chunk_cols(c)], ADD)
 
         def quantize_w2(m, after):
             codes = sb("w2_codes%d" % m, [P, P], U32)
@@ -159,7 +176,6 @@ def tile_picked_devox_relu_e_kernel(tc, xT, w1, w2, gate, emb, offs, cell, pos1,
             quantize(codes[:], scales[:], w2_bf[:, m * P:(m + 1) * P, :].rearrange("p c j -> p (c j)"))
             return codes, scales
 
-        w2_first = quantize_w2(0, "emb3")
 
         z_codes = sb("z_codes", [P, U], U32)
         z_scales = sb("z_scales", [P, U], U8)
@@ -171,12 +187,12 @@ def tile_picked_devox_relu_e_kernel(tc, xT, w1, w2, gate, emb, offs, cell, pos1,
             if c < CHUNKS - 1:
                 nc.scalar.copy(dst, src)
             else:
-                nc.scalar.copy(dst[:, 0:CHUNK // 2], src[:, 0:CHUNK // 2])
-                nc.vector.tensor_copy(dst[:, CHUNK // 2:CHUNK], src[:, CHUNK // 2:CHUNK])
-        for c in range(CHUNKS):
+                nc.vector.tensor_copy(dst, src)
+        w2_first = quantize_w2(0, "pairs3")
+        for c in (3, 0, 1, 2):
             quantize(z_codes[:, chunk_cols(c)], z_scales[:, chunk_cols(c)], z_bf[c][:])
-        y = [sb(name, [P, U], F32) for name in ("pairs3", "y1")]
-        pieces = ((0, 256, 4, False), (256, 512, 5, False), (512, 768, 6, True), (768, 896, 7, False), (896, 1024, 3, True))
+        y = [sb(name, [P, U], F32) for name in ("pairs2", "y1")]
+        pieces = ((768, 1024, 4, False), (0, 256, 5, False), (256, 512, 6, True), (512, 640, 7, False), (640, 768, 3, True))
         for lo, hi, b, on_vector in pieces:
             acc = bank(b, hi - lo)
             product(acc[:], w2_first[0][:], w2_first[1][:], z_codes[:, lo:hi], z_scales[:, lo:hi])
@@ -184,7 +200,7 @@ def tile_picked_devox_relu_e_kernel(tc, xT, w1, w2, gate, emb, offs, cell, pos1,
                 nc.vector.tensor_scalar(y[0][:, lo:hi], acc[:], 0.0, None, MAX)
             else:
                 nc.scalar.activation(y[0][:, lo:hi], acc[:], RELU)
-        w2_second = quantize_w2(1, "z_bf3")
+        w2_second = quantize_w2(1, "z_bf2")
         for a in range(2):
             cols = slice(a * (U // 2), (a + 1) * (U // 2))
             acc = bank(6 + a, U // 2)
@@ -201,17 +217,14 @@ def tile_picked_devox_relu_e_kernel(tc, xT, w1, w2, gate, emb, offs, cell, pos1,
         partial = sb("partial", [P, V], F32)
         nc.gpsimd.tensor_tensor(partial[:], weighted[0][:], weighted[1][:], ADD)
 
-        total = [bank(b, V // 2) for b in (4, 5)]
+        total = [bank(b, HALF) for b in (4, 5)]
         for d in range(D):
-            picked = sb("picked1%d" % d, [P, V], F32)
-            if d < D - 1:
-                nc.vector.tensor_copy(picked[:], y[1][:].indirect(pos_t[d][:]))
-            else:
-                for a in range(2):
-                    nc.vector.tensor_copy(picked[:, half_cols(a)], y[1][:].indirect(half_list(pos_t[d], a)))
-            scaled = sb("scaled%d" % d, [P, V], F32)
-            for a in range(2):
-                turned = bank(2 * (d % 2) + a, V // 2)
+            halves = 2 if d < D - 1 else 1
+            picked = sb("picked1%d" % d, [P, halves * HALF], F32)
+            nc.vector.tensor_copy(picked[:], y[1][:].indirect(pos_t[d][:, 0:halves * HALF // 16]))
+            scaled = sb("scaled%d" % d, [P, halves * HALF], F32)
+            for a in range(halves):
+                turned = bank(2 * (d % 2) + a, HALF)
                 for i in range(2):
                     b = 2 * a + i
                     nc.tensor.transpose(turned[:, i * P:(i + 1) * P], picked[:, b * P:(b + 1) * P], ident[:])
@@ -219,17 +232,20 @@ def tile_picked_devox_relu_e_kernel(tc, xT, w1, w2, gate, emb, offs, cell, pos1,
                     b = 2 * a + i
                     nc.scalar.activation(scaled[:, b * P:(b + 1) * P], turned[:, i * P:(i + 1) * P], COPY,
                                          scale=gate_col[d][:, b:b + 1])
-            for a in range(2):
+            for a in range(halves):
                 for i in range(2):
                     b = 2 * a + i
                     nc.tensor.matmul(total[a][:, i * P:(i + 1) * P], scaled[:, b * P:(b + 1) * P], ident[:],
-                                     start=(d == 0 and i == 0), stop=(d == D - 1 and i == 1), is_transpose=True)
+                                     start=(d == 0 and i == 0), stop=(d == D - 1 - a and i == 1), is_transpose=True)
+        res = [sb("res%d" % m, [P, V], F32) for m in range(2)]
         last = sb("weighted0", [P, V], F32)
         nc.vector.tensor_tensor(last[:], y[0][:].indirect(pos_t[D - 1][:]), gate_row[D - 1][:], MULT)
-        res = [sb("res%d" % m, [P, V], F32) for m in range(2)]
+        rest = sb("weighted1", [P, HALF], F32)
+        nc.vector.tensor_tensor(rest[:], y[1][:].indirect(half_list(pos_t[D - 1], 1)), gate_row[D - 1][:, half_cols(1)], MULT)
         for a in range(2):
-            cols = slice(a * (V // 2), (a + 1) * (V // 2))
-            nc.vector.tensor_tensor(res[0][:, cols], last[:, cols], partial[:, cols], ADD)
-            nc.sync.dma_start(out[0:P, cols], res[0][:, cols])
-            nc.scalar.copy(res[1][:, cols], total[a][:])
-            nc.scalar.dma_start(out[P:2 * P, cols], res[1][:, cols])
+            nc.vector.tensor_tensor(res[0][:, half_cols(a)], last[:, half_cols(a)], partial[:, half_cols(a)], ADD)
+            nc.sync.dma_start(out[0:P, half_cols(a)], res[0][:, half_cols(a)])
+        nc.scalar.copy(res[1][:, half_cols(0)], total[0][:])
+        nc.scalar.dma_start(out[P:2 * P, half_cols(0)], res[1][:, half_cols(0)])
+        nc.vector.tensor_tensor(res[1][:, half_cols(1)], rest[:], total[1][:], ADD)
+        nc.sync.dma_start(out[P:2 * P, half_cols(1)], res[1][:, half_cols(1)])

from contextlib import ExitStack

import concourse.mybir as mybir
from concourse.masks import make_identity

K, T, S, D, V, H, N, U = 512, 2048, 512, 3, 512, 512, 256, 1024
FLOPS = 2 * K * H * S + 2 * H * N * U

F32 = mybir.dt.float32
BF16 = mybir.dt.bfloat16
U32 = mybir.dt.uint32
U16 = mybir.dt.uint16
U8 = mybir.dt.uint8
FP8X4 = mybir.dt.float8_e4m3fn_x4
ADD = mybir.AluOpType.add
MULT = mybir.AluOpType.mult
MAX = mybir.AluOpType.max
RELU = mybir.ActivationFunctionType.Relu
COPY = mybir.ActivationFunctionType.Copy

P = 128
PACK = 4
HALF = S // 2
CHUNK = 256
CHUNKS = U // CHUNK
ORDER = (2, 0, 1, 3)


def tile_picked_devox_relu_e_kernel(tc, xT, w1, w2, gate, emb, offs, cell, pos1, pos2, pos3, out):
    nc = tc.nc
    with ExitStack() as ctx:
        keep = ctx.enter_context(tc.tile_pool(name="keep", bufs=1))
        psum = ctx.enter_context(tc.psum_pool(name="psum", bufs=1))

        def sb(name, shape, dtype):
            return keep.tile(shape, dtype, name=name, align_bytes=64)

        def bank(b, width):
            return psum.tile([P, width], F32, name="bank%d" % b)

        def load_list(name, src):
            t = keep.tile([P, S // 16], U16, name=name)
            nc.sync.dma_start(t[:], src)
            return t

        def quantize(codes, scales, values):
            nc.vector.quantize_mx(out=codes.bitcast(FP8X4), scales=scales, in_=values)

        def product(acc, w_codes, w_scales, a_codes, a_scales):
            nc.tensor.matmul_mx(out=acc, lhsT=w_codes.bitcast(FP8X4), lhsT_scale=w_scales,
                                rhs=a_codes.bitcast(FP8X4), rhs_scale=a_scales, start=True, stop=True)

        x_rows = xT.rearrange("(p j) t -> p j t", j=PACK)
        x_plane = [sb("x%d" % j, [P, T], F32) for j in range(PACK)]
        w1_rows = w1.rearrange("(p j) c -> p j c", j=PACK)
        w1_raw = [sb("w1_raw%d" % a, [P, PACK, H // 2], F32) for a in range(2)]
        nc.sync.dma_start(x_plane[0][:], x_rows[:, 0, :])
        offs_t = load_list("offs_t", offs)
        for j in range(1, PACK):
            nc.sync.dma_start(x_plane[j][:], x_rows[:, j, :])
        for a in range(2):
            nc.sync.dma_start(w1_raw[a][:], w1_rows[:, :, a * (H // 2):(a + 1) * (H // 2)])
        cell_t = load_list("cell_t", cell)
        emb_rows = emb.rearrange("(p t) r -> p t r", t=PACK)
        emb_plane = [sb("emb%d" % t, [P, U], F32) for t in range(PACK)]
        for t in ORDER:
            nc.sync.dma_start(emb_plane[t][:], emb_rows[:, t, :])
        w2_raw = sb("w2_raw", [P, PACK, N], F32)
        nc.sync.dma_start(w2_raw[:], w2.rearrange("(p j) c -> p j c", j=PACK))
        pos_t = [load_list("pos%d_t" % d, src) for d, src in enumerate((pos1, pos2, pos3))]
        gate_row = [sb("gate_row%d" % d, [P, V], F32) for d in range(D)]
        for d in range(D):
            nc.sync.dma_start(gate_row[d][:], gate[d])
        blocks = [V // P, V // P, HALF // P]
        gate_col = [sb("gate_col%d" % d, [P, blocks[d]], F32) for d in range(D)]
        with nc.allow_non_contiguous_dma("one weight a partition"):
            for d in range(D):
                nc.sync.dma_start(gate_col[d][:], gate[d, 0, 0:blocks[d] * P].rearrange("(b p) -> p b", p=P))

        ident = sb("ident", [P, P], F32)
        make_identity(nc, ident[:])

        up = [sb("up%d" % t, [P, U], F32) for t in range(PACK)]
        for t in range(PACK):
            nc.vector.memset(up[t][:], 0.0)

        x_bf = [sb("x_bf%d" % a, [P, HALF, PACK], BF16) for a in range(2)]
        x_codes = sb("x_codes", [P, S], U32)
        x_scales = sb("x_scales", [P, S], U8)

        def half_cols(a):
            return slice(a * HALF, (a + 1) * HALF)

        def half_list(lst, a):
            return lst[:, a * (HALF // 16):(a + 1) * (HALF // 16)]

        for j in range(PACK):
            for a in range(2):
                nc.vector.tensor_copy(x_bf[a][:, :, j], x_plane[j][:].indirect(half_list(offs_t, a)))
                if j == PACK - 1:
                    quantize(x_codes[:, half_cols(a)], x_scales[:, half_cols(a)],
                             x_bf[a][:].rearrange("p n j -> p (n j)"))

        w1_bf = sb("w1_bf", [P, PACK * H], BF16)
        w1_dealt = w1_bf[:].rearrange("p (t m j) -> p m t j", t=PACK, j=PACK)
        w1_early = w1_raw[0][:].rearrange("p j (m t) -> p m t j", t=PACK)
        w1_late = w1_raw[1][:].rearrange("p j (m t) -> p m t j", t=PACK)
        w1_codes = sb("w1_codes", [P, H], U32)
        w1_scales = sb("w1_scales", [P, H], U8)
        def quantize_w1(lo, hi):
            quantize(w1_codes[:, lo * P:hi * P], w1_scales[:, lo * P:hi * P], w1_bf[:, lo * H:hi * H])

        for lo, hi in ((2, 3), (0, 2), (3, 4)):
            nc.scalar.copy(w1_dealt[:, 0:P // 2, lo:hi], w1_early[:, :, lo:hi])
        nc.vector.tensor_copy(w1_dealt[:, P // 2:P, 2:3], w1_late[:, :, 2:3])
        quantize_w1(2, 3)
        nc.vector.tensor_copy(w1_dealt[:, P // 2:P, 3:4], w1_late[:, :, 3:4])
        nc.vector.tensor_copy(w1_dealt[:, P // 2:P, 0:2], w1_late[:, :, 0:2])
        quantize_w1(0, 2)
        quantize_w1(3, 4)

        h = [sb("h%d" % t, [P, S], F32) for t in range(PACK)]
        first = ORDER[0]
        cols = slice(first * P, (first + 1) * P)
        for a in range(2):
            acc = bank(a, HALF)
            product(acc[:], w1_codes[:, cols], w1_scales[:, cols], x_codes[:, half_cols(a)], x_scales[:, half_cols(a)])
            nc.scalar.activation(h[first][:, half_cols(a)], acc[:], RELU)
            nc.vector.tensor_copy(up[first][:].indirect(half_list(cell_t, a)), h[first][:, half_cols(a)])
        for i, t in enumerate(ORDER[1:]):
            acc = bank(2 + i, S)
            cols = slice(t * P, (t + 1) * P)
            product(acc[:], w1_codes[:, cols], w1_scales[:, cols], x_codes[:], x_scales[:])
            nc.scalar.activation(h[t][:], acc[:], RELU)
            nc.vector.tensor_copy(up[t][:].indirect(cell_t[:]), h[t][:])

        def chunk_cols(c):
            return slice(c * CHUNK, (c + 1) * CHUNK)

        w2_bf = sb("w2_bf", [P, N, PACK], BF16)
        nc.scalar.copy(w2_bf[:], w2_raw[:].rearrange("p j c -> p c j"))

        emb_turned = sb("emb_turned", [P, (CHUNKS - 1) * CHUNK], F32)
        emb_psum = []
        for c in range(CHUNKS - 1):
            there = bank(5 + c, CHUNK)
            back = bank(c, CHUNK)
            for i in range(2):
                b = 2 * c + i
                nc.tensor.transpose(there[:, i * P:(i + 1) * P], emb_plane[3][:, b * P:(b + 1) * P], ident[:])
            nc.scalar.copy(emb_turned[:, chunk_cols(c)], there[:])
            for i in range(2):
                b = 2 * c + i
                nc.tensor.transpose(back[:, i * P:(i + 1) * P], emb_turned[:, b * P:(b + 1) * P], ident[:])
            emb_psum.append(back)

        z_plane = [sb("z_plane%d" % t, [P, U], BF16) for t in range(PACK - 1)]
        pairs = [sb("pairs%d" % c, [P, 2, CHUNK, 2], BF16) for c in range(CHUNKS)]
        nc.gpsimd.tensor_tensor(z_plane[2][:], up[2][:], emb_plane[2][:], ADD)
        for c in range(CHUNKS):
            nc.scalar.copy(pairs[c][:, 1, :, :], z_plane[2][:, chunk_cols(c)].unsqueeze(2).to_broadcast([P, CHUNK, 2]))
        for t in range(2):
            for a in range(1 + t):
                cols = slice(a * (U // (1 + t)), (a + 1) * (U // (1 + t)))
                nc.gpsimd.tensor_tensor(z_plane[t][:, cols], up[t][:, cols], emb_plane[t][:, cols], ADD)
            for c in range(CHUNKS):
                nc.scalar.copy(pairs[c][:, 0, :, t], z_plane[t][:, chunk_cols(c)])
        for c in range(CHUNKS - 1):
            nc.vector.tensor_tensor(pairs[c][:, 1, :, 1], up[3][:, chunk_cols(c)], emb_psum[c][:], ADD)
        c = CHUNKS - 1
        nc.gpsimd.tensor_tensor(pairs[c][:, 1, :, 1], up[3][:, chunk_cols(c)], emb_plane[3][:, chunk_cols(c)], ADD)

        def quantize_w2(m, after):
            codes = sb("w2_codes%d" % m, [P, P], U32)
            scales = sb(after, [P, P], U8)
            quantize(codes[:], scales[:], w2_bf[:, m * P:(m + 1) * P, :].rearrange("p c j -> p (c j)"))
            return codes, scales


        z_codes = sb("z_codes", [P, U], U32)
        z_scales = sb("z_scales", [P, U], U8)
        z_bf = [sb("z_plane1" if c == 0 else "z_bf%d" % c, [P, PACK * CHUNK], BF16) for c in range(CHUNKS)]
        for c in range(CHUNKS):
            words = pairs[c][:].rearrange("p u r e -> p (u r e)").bitcast(F32)
            src = words.rearrange("p (u r) -> p r u", u=2)
            dst = z_bf[c][:].bitcast(F32).rearrange("p (r u) -> p r u", u=2)
            if c < CHUNKS - 1:
                nc.scalar.copy(dst, src)
            else:
                nc.vector.tensor_copy(dst, src)
        w2_first = quantize_w2(0, "pairs3")
        for c in (3, 0, 1, 2):
            quantize(z_codes[:, chunk_cols(c)], z_scales[:, chunk_cols(c)], z_bf[c][:])
        y = [sb(name, [P, U], F32) for name in ("pairs2", "y1")]
        pieces = ((768, 1024, 4, False), (0, 256, 5, False), (256, 512, 6, True), (512, 640, 7, False), (640, 768, 3, True))
        for lo, hi, b, on_vector in pieces:
            acc = bank(b, hi - lo)
            product(acc[:], w2_first[0][:], w2_first[1][:], z_codes[:, lo:hi], z_scales[:, lo:hi])
            if on_vector:
                nc.vector.tensor_scalar(y[0][:, lo:hi], acc[:], 0.0, None, MAX)
            else:
                nc.scalar.activation(y[0][:, lo:hi], acc[:], RELU)
        w2_second = quantize_w2(1, "z_bf2")
        for a in range(2):
            cols = slice(a * (U // 2), (a + 1) * (U // 2))
            acc = bank(6 + a, U // 2)
            product(acc[:], w2_second[0][:], w2_second[1][:], z_codes[:, cols], z_scales[:, cols])
            nc.scalar.activation(y[1][:, cols], acc[:], RELU)

        weighted = []
        for d in range(D - 1):
            picked = sb("picked0%d" % d, [P, V], F32)
            nc.vector.tensor_copy(picked[:], y[0][:].indirect(pos_t[d][:]))
            w = sb("weighted%d" % d, [P, V], F32)
            nc.gpsimd.tensor_tensor(w[:], picked[:], gate_row[d][:], MULT)
            weighted.append(w)
        partial = sb("partial", [P, V], F32)
        nc.gpsimd.tensor_tensor(partial[:], weighted[0][:], weighted[1][:], ADD)

        total = [bank(b, HALF) for b in (4, 5)]
        for d in range(D):
            halves = 2 if d < D - 1 else 1
            picked = sb("picked1%d" % d, [P, halves * HALF], F32)
            nc.vector.tensor_copy(picked[:], y[1][:].indirect(pos_t[d][:, 0:halves * HALF // 16]))
            scaled = sb("scaled%d" % d, [P, halves * HALF], F32)
            for a in range(halves):
                turned = bank(2 * (d % 2) + a, HALF)
                for i in range(2):
                    b = 2 * a + i
                    nc.tensor.transpose(turned[:, i * P:(i + 1) * P], picked[:, b * P:(b + 1) * P], ident[:])
                for i in range(2):
                    b = 2 * a + i
                    nc.scalar.activation(scaled[:, b * P:(b + 1) * P], turned[:, i * P:(i + 1) * P], COPY,
                                         scale=gate_col[d][:, b:b + 1])
            for a in range(halves):
                for i in range(2):
                    b = 2 * a + i
                    nc.tensor.matmul(total[a][:, i * P:(i + 1) * P], scaled[:, b * P:(b + 1) * P], ident[:],
                                     start=(d == 0 and i == 0), stop=(d == D - 1 - a and i == 1), is_transpose=True)
        res = [sb("res%d" % m, [P, V], F32) for m in range(2)]
        last = sb("weighted0", [P, V], F32)
        nc.vector.tensor_tensor(last[:], y[0][:].indirect(pos_t[D - 1][:]), gate_row[D - 1][:], MULT)
        rest = sb("weighted1", [P, HALF], F32)
        nc.vector.tensor_tensor(rest[:], y[1][:].indirect(half_list(pos_t[D - 1], 1)), gate_row[D - 1][:, half_cols(1)], MULT)
        for a in range(2):
            nc.vector.tensor_tensor(res[0][:, half_cols(a)], last[:, half_cols(a)], partial[:, half_cols(a)], ADD)
            nc.sync.dma_start(out[0:P, half_cols(a)], res[0][:, half_cols(a)])
        nc.scalar.copy(res[1][:, half_cols(0)], total[0][:])
        nc.scalar.dma_start(out[P:2 * P, half_cols(0)], res[1][:, half_cols(0)])
        nc.vector.tensor_tensor(res[1][:, half_cols(1)], rest[:], total[1][:], ADD)
        nc.sync.dma_start(out[P:2 * P, half_cols(1)], res[1][:, half_cols(1)])
